import numpy as np
import ml_dtypes


def mxq(x, axis, fmt="e4m3"):
    dtype, down = {"e4m3": (ml_dtypes.float8_e4m3fn, 7), "e5m2": (ml_dtypes.float8_e5m2, 14)}[fmt]
    v = np.moveaxis(np.asarray(x, np.float32).astype(ml_dtypes.bfloat16).astype(np.float64), axis, -1)
    blocks = v.reshape(v.shape[:-1] + (-1, 32))
    amax = np.abs(blocks).max(-1, keepdims=True)
    byte = np.maximum(np.where(amax > 0, np.frexp(amax)[1] - 1 + 127, 0) - down, 1)
    scale = np.exp2(byte - 127.0)
    codes = (blocks / scale).astype(np.float32).astype(dtype).astype(np.float64)
    return np.moveaxis((codes * scale).reshape(v.shape), -1, axis)


WIDE = False


def mx_kscale(k):
    if not WIDE:
        return np.ones(k)
    levels = np.array([10, -10, 5, -5, 0])
    if k % 512:
        return np.exp2(np.random.permutation(np.resize(levels, k // 32))).repeat(32)
    a = np.empty((k // 512, 16))
    for p in range(k // 512):
        a[p, :8] = np.random.permutation(np.resize(levels, 8))
        for g in range(8):
            far = levels[np.abs(levels - a[p, g]) >= 10]
            a[p, g + 8] = far[np.random.randint(len(far))]
    return np.exp2(a.ravel()).repeat(32)


BF16 = ml_dtypes.bfloat16


def bf(x):
    return np.asarray(x, np.float32).astype(BF16)


def f64(x):
    return np.asarray(x).astype(np.float64)


E2M1 = np.array([0.0, 0.5, 1.0, 1.5, 2.0, 3.0, 4.0, 6.0, -0.0, -0.5, -1.0, -1.5, -2.0, -3.0, -4.0, -6.0])


def pack_weight(w, fmt):
    k, n = w.shape
    w = f64(bf(w)).reshape(k // 32, 32, n)
    amax = np.abs(w).max(1)
    if fmt == "e4m3":
        byte = np.frexp(amax)[1] - 1 + 127 - 7
    else:
        mant, ex = np.frexp(amax / 6.0)
        byte = np.where(mant > 0.5, ex, ex - 1) + 127
    byte = np.clip(np.where(amax > 0, byte, 1), 1, 254)
    scaled = (w * np.exp2(127.0 - byte)[:, None, :]).reshape(k, n).astype(np.float32)
    by_word = np.ascontiguousarray(scaled.reshape(k // 512, 128, 4, n).transpose(0, 1, 3, 2))
    if fmt == "e4m3":
        words = by_word.astype(ml_dtypes.float8_e4m3fn).view(np.uint8)
    else:
        c = by_word.astype(ml_dtypes.float4_e2m1fn).view(np.uint8) & 0xF
        words = c[..., 0::2] | (c[..., 1::2] << 4)
    return np.ascontiguousarray(words), np.ascontiguousarray(byte.astype(np.uint8).reshape(k // 512, 16, n))


def unpack_weight(words, scales, fmt):
    g, p, n, _ = words.shape
    if fmt == "e4m3":
        vals = np.ascontiguousarray(words).view(ml_dtypes.float8_e4m3fn).astype(np.float64)
    else:
        nib = np.empty((g, p, n, 4), np.uint8)
        nib[..., 0::2] = words & 0xF
        nib[..., 1::2] = words >> 4
        vals = E2M1[nib]
    vals = vals * np.repeat(np.exp2(scales.astype(np.float64) - 127.0), 8, axis=1)[..., None]
    return vals.transpose(0, 1, 3, 2).reshape(g * 512, n)
def pack4(w):
    words, scales = pack_weight(w, "e2m1")
    return words.reshape(words.shape[0], 128, -1), scales


def unpack4(words, scales):
    return unpack_weight(words.reshape(words.shape[0], 128, -1, 2), scales, "e2m1")


M, K, Z, D, T = 512, 1024, 4, 1024, 512


def sigmoid(v):
    return 1.0 / (1.0 + np.exp(-v))


def setup_inputs():
    s, t = mx_kscale(K), mx_kscale(D)
    x = np.random.standard_normal((M, K)) * s
    phi = 0.5 * np.random.standard_normal((M, D)) * t
    w_psi = np.random.standard_normal((K, Z * D)) / np.sqrt(K) / s[:, None] * np.tile(t, Z)
    b_psi = 0.3 * np.random.standard_normal((Z, D)) * t
    w_gamma = np.random.standard_normal((K, D)) / np.sqrt(K) / s[:, None]
    b_gamma = 1.0 + 0.3 * np.random.standard_normal(D)
    w_pref = 2.0 * np.random.standard_normal((D, T)) / np.sqrt(D) / t[:, None]
    beta = 2.0 + 0.3 * np.random.standard_normal(T)
    psi_words, psi_scales = pack4(w_psi)
    gamma_words, gamma_scales = pack4(w_gamma)
    pref_words, pref_scales = pack4(w_pref)
    return {"x": bf(x), "phi": bf(phi),
            "psi_words": psi_words, "psi_scales": psi_scales, "b_psi": bf(b_psi),
            "gamma_words": gamma_words, "gamma_scales": gamma_scales, "b_gamma": bf(b_gamma),
            "pref_words": pref_words, "pref_scales": pref_scales, "beta": bf(beta)}


def reference(x, phi, psi_words, psi_scales, b_psi, gamma_words, gamma_scales, b_gamma, pref_words, pref_scales, beta):
    xq = mxq(f64(x), 1, "e4m3")
    future = (xq @ unpack4(psi_words, psi_scales)).reshape(M, Z, D) + f64(b_psi)
    future = np.maximum(future, 0.0)
    gamma = sigmoid((xq @ unpack4(gamma_words, gamma_scales)) + f64(b_gamma))
    psi = f64(phi)[:, None, :] + gamma[:, None, :] * future
    val = (mxq(psi.reshape(M * Z, D), 1, "e4m3") @ unpack4(pref_words, pref_scales)).reshape(M, Z, T)
    best = np.max(val, axis=1)
    e = np.exp(f64(beta) * (val - best[:, None, :]))
    soft = np.sum(e * val, axis=1) / np.sum(e, axis=1)
    return best, soft

@@ -1,0 +1,426 @@
+from contextlib import ExitStack
+
+import concourse.mybir as mybir
+from concourse.masks import make_identity
+
+M, K, Z, D, T = 512, 1024, 4, 1024, 512
+FLOPS = 2 * M * K * (Z * D + D) + 2 * M * Z * D * T
+
+F32 = mybir.dt.float32
+BF16 = mybir.dt.bfloat16
+I32 = mybir.dt.int32
+U32 = mybir.dt.uint32
+U8 = mybir.dt.uint8
+FP8X4 = mybir.dt.float8_e4m3fn_x4
+FP4X4 = mybir.dt.float4_e2m1fn_x4
+ALU = mybir.AluOpType
+ACT = mybir.ActivationFunctionType
+
+P = 128
+W = 512
+
+
+def cols(i, n):
+    return slice(i * n, (i + 1) * n)
+
+
+def tile_successor_feature_gpi_f1_kernel(
+    tc, x, phi, psi_words, psi_scales, b_psi, gamma_words, gamma_scales, b_gamma,
+    pref_words, pref_scales, beta, out_0, out_1,
+):
+    nc = tc.nc
+    with ExitStack() as ctx:
+        sb = ctx.enter_context(tc.tile_pool(name="sb", bufs=1))
+        ps = ctx.enter_context(tc.psum_pool(name="ps", bufs=1))
+        ctx.enter_context(tc.manual_schedule())
+
+        def new(name, shape, dtype):
+            return sb.tile(shape, dtype, name=name, align_bytes=64)
+
+        bank = [ps.tile([P, W], F32, name="bank%d" % i) for i in range(8)]
+
+        groups = [(None, 0), (0, 0), (1, 0), (2, 0), (3, 0), (None, 1), (0, 1), (1, 1), (2, 1), (3, 1)]
+
+        ident = new("ident", [P, P], F32)
+        ident_bf = new("ident_bf", [P, P], BF16)
+        x_sb = [new("x_sb%d" % i, [P, K], BF16) for i in range(4)]
+        x_t = [new("x_t%d" % i, [P, K], BF16) for i in range(4)]
+        x_codes = new("x_codes", [P, 2, M], U32)
+        x_plane = new("x_plane", [P, 2, M], U8)
+        w_perm = [new("w_perm%d" % i, [P, 2, 2 * W], U8) for i in range(3)]
+        plane_perm = [new("plane_perm%d" % i, [P, 2, W], U8) for i in range(3)]
+        warm = new("warm", [P, W], BF16)
+        phi_sb = [new("phi_sb%d" % g, [P, 4, W], BF16) for g in range(2)]
+        phi_t = [new("phi_t%d" % g, [P, 4 * W], BF16) for g in range(2)]
+        w_sb = [new("w_sb%d" % i, [P, 2, 2 * W], U8) for i in range(10)]
+        pref_sb = new("pref_sb", [P, 2, 2 * T], U8)
+        gamma_plane = new("gamma_plane", [P, 2, D], U8)
+        psi_plane = [new("psi_plane%d" % i, [P, 2, 2 * D], U8) for i in range(2)]
+        pref_plane = new("pref_plane", [P, 2, T], U8)
+        rows = new("rows", [P, 640], BF16)
+        rows_p = new("rows_p", [P, 640], BF16)
+        consts = new("consts", [P, 5, 16], F32)
+        dummy = new("dummy", [P, 8], F32)
+        s_sb = [new("s_sb%d" % i, [P, 4 * W], F32) for i in range(4)]
+        gate = [new("gate%d" % g, [P, 4 * W], F32) for g in range(2)]
+        t1 = [new("t1_%d" % i, [P, 4 * W], F32) for i in range(2)]
+        psi_bf = [new("psi_bf%d" % i, [P, 4 * W], BF16) for i in range(4)]
+        psi_codes = [[new("psi_codes%d%d" % (g, i), [P, W], U32) for i in range(4)] for g in range(2)]
+        psi_qplane = [[new("psi_qplane%d%d" % (g, i), [P, W], U8) for i in range(4)] for g in range(2)]
+        best = [new("best%d" % i, [P, P], F32) for i in range(8)]
+        diff = [tile[:].bitcast(F32) for tile in x_sb + x_t]
+        expo = [s_sb[i // 4][:, cols(i % 4, W)] for i in range(8)]
+        wval = [s_sb[2 + i // 4][:, cols(i % 4, W)] for i in range(8)]
+        num_sb = [gate[1][:, cols(i, W)] for i in range(2)]
+        pair_sb = [new("pair_sb%d" % i, [P, 2, W], F32) for i in range(4)]
+        relu_sb = [new("relu_sb%d" % i, [P, W], F32) for i in range(3)]
+        rsq = [new("rsq%d" % i, [P, W], F32) for i in range(2)]
+        rec = [new("rec%d" % i, [P, W], F32) for i in range(2)]
+        half = [new("half%d" % i, [P, W], F32) for i in range(2)]
+        soft_out = [gate[0][:, cols(i, W)] for i in range(4)]
+
+        def load_scales(plane, src, c0, c1):
+            view = src.bitcast(I32).rearrange("k (q r) n -> r q k n", r=4)
+            for r in range(4):
+                nc.sync.dma_start(out=plane[r:P:32, :, :].bitcast(I32), in_=view[r][:, :, c0 // 4 : c1 // 4])
+
+        def load_words(i):
+            z, g = groups[i]
+            if z is None:
+                src, c0 = gamma_words, g * W
+            else:
+                src, c0 = psi_words, z * D + g * W
+            view = src.bitcast(I32).rearrange("k p n -> p k n")
+            nc.sync.dma_start(out=w_sb[i][:].bitcast(I32), in_=view[:, :, c0 // 2 : (c0 + W) // 2])
+
+        def load_phi(g):
+            nc.sync.dma_start(out=phi_sb[g][:], in_=phi[:, cols(g, W)].rearrange("(a p) c -> p a c", p=P))
+
+        def clear(eng, plane):
+            eng.memset(plane[:].rearrange("p k n -> p (k n)").bitcast(U32), 0)
+
+        nc.vector.memset(rows[:], 0.0)
+        nc.vector.memset(dummy[:], 0.0)
+        nc.vector.memset(warm[:], 0.0)
+        clear(nc.vector, gamma_plane)
+        clear(nc.vector, psi_plane[0])
+        clear(nc.vector, psi_plane[1])
+        clear(nc.vector, pref_plane)
+        make_identity(nc, ident[:])
+        make_identity(nc, ident_bf[:])
+
+        nc.sync.dma_start(out=x_sb[0][:], in_=x[cols(0, P), :])
+        nc.sync.dma_start(out=x_sb[1][:], in_=x[cols(1, P), :])
+        nc.sync.dma_start(out=x_sb[2][:], in_=x[cols(2, P), :])
+        nc.sync.dma_start(out=x_sb[3][:], in_=x[cols(3, P), :])
+        nc.scalar.dma_start(out=rows[0:8, 0:W], in_=b_psi.rearrange("z (g c) -> (z g) c", g=2))
+        nc.scalar.dma_start(out=rows[8:10, 0:W], in_=b_gamma.rearrange("(g c) -> g c", g=2))
+        nc.scalar.dma_start(out=rows[0:4, W : W + P], in_=beta.rearrange("(a c) -> a c", a=4))
+        nc.scalar.activation(out=dummy[:, 4:5], in_=dummy[:, 0:1], func=ACT.Sigmoid)
+        load_words(0)
+        load_scales(gamma_plane, gamma_scales, 0, D)
+        load_scales(psi_plane[0], psi_scales, 0, 2 * D)
+        load_words(1)
+        load_words(2)
+        load_phi(0)
+        load_scales(psi_plane[1], psi_scales, 2 * D, Z * D)
+        for i in (3, 4, 5, 6):
+            load_words(i)
+        load_phi(1)
+        for i in (7, 8, 9):
+            load_words(i)
+        load_scales(pref_plane, pref_scales, 0, T)
+        nc.sync.dma_start(out=pref_sb[:].bitcast(I32), in_=pref_words.bitcast(I32).rearrange("k p n -> p k n"))
+
+        def word_copy(eng_copy, dst, src):
+            eng_copy(out=dst.bitcast(F32).rearrange("p (a m u) -> p a m u", a=2, u=2),
+                     in_=src.rearrange("p (a u m) -> p a m u", a=2, u=2))
+
+        def x_transpose(a):
+            words = x_sb[a][:].bitcast(F32)
+            for k in range(2):
+                for u in range(2):
+                    nc.tensor.transpose(bank[4 + a][:, cols(2 * k + u, P)], words[:, 256 * k + u : 256 * (k + 1) : 2], ident[:])
+            word_copy(nc.scalar.copy, x_t[a][:], bank[4 + a][:])
+
+        def x_quant(a):
+            for k in range(2):
+                nc.vector.quantize_mx(out=x_codes[:, k, cols(a, P)].bitcast(FP8X4), scales=x_plane[:, k, cols(a, P)],
+                                      in_=x_t[a][:, cols(k, W)])
+
+        def const_setup():
+            view = bank[0][:].bitcast(BF16)
+            for j in range(5):
+                nc.tensor.transpose(view[:, cols(j, P)], rows_p[:, cols(j, P)], ident_bf[:])
+            nc.scalar.copy(out=consts[:], in_=view[:, 0 : 5 * P].rearrange("p (j c) -> p j c", j=5)[:, :, 0:16])
+
+        def w_plane(i):
+            z, g = groups[i]
+            if z is None:
+                return gamma_plane[:, :, cols(g, W)]
+            return psi_plane[z // 2][:, :, cols(2 * (z % 2) + g, W)]
+
+        def permute_words(i, k):
+            nc.vector.tensor_copy(out=w_perm[i][:, k, :].rearrange("p (t c b) -> p t c b", t=4, b=2),
+                                  in_=w_sb[i][:, k, :].rearrange("p (c t b) -> p t c b", t=4, b=2))
+
+        def permute_scales(i):
+            nc.vector.tensor_copy(out=plane_perm[i][:].rearrange("p k (t c) -> p k t c", t=4),
+                                  in_=w_plane(i).rearrange("p k (c t) -> p k t c", t=4))
+
+        def warm_up(n):
+            for j in range(n):
+                nc.tensor.matmul(out=bank[1][:], lhsT=warm[:, 0:P], rhs=warm[:], start=True, stop=True)
+
+        warm_up(4)
+        x_transpose(0)
+        nc.vector.tensor_copy(out=rows_p[:, 0:W].rearrange("p (t c) -> p t c", t=4),
+                              in_=rows[:, 0:W].rearrange("p (c t) -> p t c", t=4))
+        nc.vector.tensor_copy(out=rows_p[:, W : W + P], in_=rows[:, W : W + P])
+        x_transpose(1)
+        x_quant(0)
+        x_transpose(2)
+        x_quant(1)
+        permute_words(0, 0)
+        x_transpose(3)
+        const_setup()
+        warm_up(3)
+        x_quant(2)
+        permute_words(0, 1)
+        x_quant(3)
+        permute_scales(0)
+        permute_scales(1)
+        permute_words(1, 0)
+        permute_words(1, 1)
+
+        count = {"mx": 1, "tr": 0, "relu": 0}
+        OFFLOAD = []
+
+        def take(kind):
+            b = bank[count[kind] % 4 + (0 if kind == "mx" else 4)]
+            count[kind] += 1
+            return b
+
+        def stage1_mx(i, h):
+            for a in (2 * h, 2 * h + 1):
+                acc = take("mx")
+                for k in range(2):
+                    nc.tensor.matmul_mx(
+                        out=acc[:], lhsT=x_codes[:, k, cols(a, P)].bitcast(FP8X4), lhsT_scale=x_plane[:, k, cols(a, P)],
+                        rhs=w_sb[i][:, k, :].bitcast(FP4X4), rhs_scale=w_plane(i)[:, k, :], start=(k == 0), stop=(k == 1))
+                nc.scalar.copy(out=s_sb[i % 4][:, cols(a, W)].rearrange("q (t p) -> q t p", t=4),
+                               in_=acc[:].rearrange("q (p t) -> q t p", t=4))
+
+        def phi_turn(g, eng_copy):
+            for h in range(2):
+                b = take("mx")
+                for a in range(2):
+                    words = phi_sb[g][:, 2 * h + a, :].bitcast(F32)
+                    for u in range(2):
+                        nc.tensor.transpose(b[:, cols(2 * a + u, P)], words[:, u:256:2], ident[:])
+                word_copy(eng_copy, phi_t[g][:, cols(h, 2 * W)], b[:])
+
+        def psi_index(i):
+            z, g = groups[i]
+            return 4 * g + z
+
+        def finish_psi(n, a):
+            g, z = divmod(n, 4)
+            if (n, a) in OFFLOAD:
+                r = relu_sb[count["relu"] % 3]
+                count["relu"] += 1
+                nc.scalar.activation(out=r[:].rearrange("p (m t) -> p m t", t=4),
+                                     in_=t1[n % 2][:].rearrange("p (t m) -> p m t", t=4)[:, cols(a, P), :], func=ACT.Relu)
+                nc.gpsimd.tensor_tensor(out=psi_bf[a][:, cols(z, W)], in0=r[:], in1=phi_t[g][:, cols(a, W)], op=ALU.add)
+                return
+            nc.vector.scalar_tensor_tensor(
+                out=psi_bf[a][:, cols(z, W)].rearrange("p (m t) -> p m t", t=4),
+                in0=t1[n % 2][:].rearrange("p (t m) -> p m t", t=4)[:, cols(a, P), :],
+                scalar=0.0,
+                in1=phi_t[g][:, cols(a, W)].rearrange("p (m t) -> p m t", t=4),
+                op0=ALU.max, op1=ALU.add)
+
+        def psi_quant(g, a):
+            nc.vector.quantize_mx(out=psi_codes[g][a][:].bitcast(FP8X4), scales=psi_qplane[g][a][:], in_=psi_bf[a][:])
+
+        def consume(i, t, b):
+            z, g = groups[i]
+            if z is None:
+                nc.scalar.activation(out=gate[g][:, cols(t, W)], in_=b[:], func=ACT.Sigmoid,
+                                     bias=consts[:, t, 8 + g : 9 + g])
+                return
+            n = 4 * g + z
+            nc.vector.scalar_tensor_tensor(
+                out=t1[n % 2][:, cols(t, W)], in0=b[:], scalar=consts[:, t, 2 * z + g : 2 * z + g + 1],
+                in1=gate[g][:, cols(t, W)], op0=ALU.add, op1=ALU.mult)
+            if n == 4 and t > 0:
+                psi_quant(0, t - 1)
+            if n == 5 and t == 0:
+                psi_quant(0, 3)
+            if 1 < n < 7 or (n == 7 and t == 1):
+                finish_psi(n - 1, t if n < 7 else 0)
+
+        def stage1_turn(i, h):
+            taken = []
+            for t in (2 * h, 2 * h + 1):
+                b = take("tr")
+                taken.append((t, b))
+                for a in range(4):
+                    nc.tensor.transpose(b[:, cols(a, P)], s_sb[i % 4][:, cols(4 * a + t, P)], ident[:])
+            for t, b in taken:
+                consume(i, t, b)
+
+        def stage1_direct(i, t):
+            b = take("mx" if i == 0 else "tr")
+            for k in range(2):
+                nc.tensor.matmul_mx(
+                    out=b[:], lhsT=w_perm[i][:, k, cols(t, 2 * P)].bitcast(FP4X4), lhsT_scale=plane_perm[i][:, k, cols(t, P)],
+                    rhs=x_codes[:, k, :].bitcast(FP8X4), rhs_scale=x_plane[:, k, :], start=(k == 0), stop=(k == 1))
+            consume(i, t, b)
+
+        order = ("D00 D01 D10 S2 D02 D11 W20 D03 D12 W21 D13 P0 D20 F00 M3a D21 F01 M3b D22 F02 D23 F03 M4a "
+                 "T3a M4b T3b M5a M5b T4a M6a T5a T4b M6b T5b E "
+                 "T6a P1 M7a T6b M7b T7a M8a T7b M8b T8a M9a T8b M9b T9a T9b").split()
+        for tok in order:
+            if tok == "E":
+                nc.scalar.activation(out=dummy[:, 5:6], in_=dummy[:, 0:1], func=ACT.Exp)
+            elif tok[0] == "P":
+                phi_turn(int(tok[1]), nc.scalar.copy)
+            elif tok[0] == "S":
+                permute_scales(int(tok[1]))
+            elif tok[0] == "W":
+                permute_words(int(tok[1]), int(tok[2]))
+            elif tok[0] == "D":
+                stage1_direct(int(tok[1]), int(tok[2]))
+            elif tok[0] == "F":
+                finish_psi(int(tok[1]), int(tok[2]))
+            elif tok[0] == "M":
+                stage1_mx(int(tok[1]), "ab".index(tok[2]))
+            else:
+                stage1_turn(int(tok[1]), "ab".index(tok[2]))
+
+        NUM = (4, 5)
+        PAIR = (6, 7)
+
+        def val_mx(u, halves=(0, 1)):
+            a, j = divmod(u, 4)
+            for g in halves:
+                nc.tensor.matmul_mx(
+                    out=bank[u % 4][:], lhsT=pref_sb[:, g, cols(j, 2 * P)].bitcast(FP4X4), lhsT_scale=pref_plane[:, g, cols(j, P)],
+                    rhs=psi_codes[g][a][:].bitcast(FP8X4), rhs_scale=psi_qplane[g][a][:], start=(g == 0), stop=(g == 1))
+
+        def max_all(u):
+            nc.vector.tensor_reduce(out=best[u % 8][:], in_=bank[u % 4][:].rearrange("p (z m) -> p m z", z=4),
+                                    axis=mybir.AxisListType.X, op=ALU.max)
+
+        def subtract(u):
+            nc.vector.tensor_tensor(
+                out=diff[u % 8].rearrange("p (z m) -> p z m", z=4),
+                in0=bank[u % 4][:].rearrange("p (z m) -> p z m", z=4),
+                in1=best[u % 8][:].unsqueeze(1).to_broadcast([P, 4, P]), op=ALU.subtract)
+
+        def exponent(u):
+            j = u % 4
+            nc.scalar.activation(out=expo[u % 8], in_=diff[u % 8], func=ACT.Exp, scale=consts[:, 4, j : j + 1])
+
+        def weigh(u):
+            eng = nc.vector if u in ON_VECTOR else nc.gpsimd
+            eng.tensor_tensor(out=wval[u % 8], in0=diff[u % 8], in1=expo[u % 8], op=ALU.mult)
+
+        def sum_turn(u):
+            a, j = divmod(u, 4)
+            pair = bank[PAIR[j // 2]]
+            nc.tensor.transpose(pair[:, cols(j % 2, P)], best[u % 8][:], ident[:])
+            for dst, src in ((pair[:, cols(2 + j % 2, P)], expo[u % 8]), (bank[NUM[a % 2]][:, cols(j, P)], wval[u % 8])):
+                for z in range(4):
+                    nc.tensor.matmul(out=dst, lhsT=src[:, cols(z, P)], rhs=ident[:],
+                                     start=(z == 0), stop=(z == 3), is_transpose=True)
+
+        def halves(ap, hs):
+            return ap.rearrange("p (h c) -> p h c", h=2)[:, hs, :]
+
+        def empty(v, eng_copy):
+            a, h = divmod(v, 2)
+            eng_copy(out=pair_sb[a][:, h, :], in_=bank[PAIR[h]][:])
+            nc.sync.dma_start(out=out_0[cols(a, P), cols(h, 256)], in_=pair_sb[a][:, h, 0:256])
+
+        def empty_num(a):
+            nc.scalar.copy(out=num_sb[a], in_=bank[NUM[a]][:])
+
+        def root(a, hs):
+            nc.scalar.activation(out=halves(rsq[a % 2][:], hs), in_=pair_sb[a][:, hs, 256:W], func=ACT.Abs_reciprocal_sqrt)
+
+        def square(a, hs):
+            nc.scalar.activation(out=halves(rec[a % 2][:], hs), in_=halves(rsq[a % 2][:], hs), func=ACT.Square)
+
+        def normalise(a, hs):
+            num = num_sb[a] if a < 2 else bank[NUM[a % 2]][:]
+            nc.vector.tensor_tensor(out=halves(half[a % 2][:], hs), in0=halves(num, hs), in1=halves(rec[a % 2][:], hs), op=ALU.mult)
+
+        def finish(a, hs):
+            nc.vector.tensor_tensor(out=halves(soft_out[a], hs), in0=halves(half[a % 2][:], hs), in1=pair_sb[a][:, hs, 0:256], op=ALU.add)
+            nc.sync.dma_start(out=halves(out_1[cols(a, P), :], hs), in_=halves(soft_out[a], hs))
+
+        ON_VECTOR = (14, 15)
+        whole = slice(0, 2)
+        for u in range(4):
+            val_mx(u, (0,))
+        finish_psi(6, 1)
+        finish_psi(7, 0)
+        finish_psi(7, 1)
+        psi_quant(1, 0)
+        for u in range(4):
+            val_mx(u, (1,))
+        psi_quant(1, 1)
+        finish_psi(6, 2)
+        max_all(0)
+        extra = {0: "F72", 1: "F63", 2: "Q2", 3: "F73", 5: "Q3"}
+        steps = {1: "X4 R0", 3: "X6 R1 R2", 5: "E0 X8 R3 R4", 7: "E1 X10 R5", 8: "N0", 9: "E2 X12 R6 R7",
+                 11: "E3 X14 R8", 12: "N1 R9", 13: "R10", 14: "R11"}
+        for s in range(16):
+            if s + 1 < 16:
+                max_all(s + 1)
+            for tok in extra.get(s, "").split():
+                if tok[0] == "F":
+                    finish_psi(int(tok[1]), int(tok[2]))
+                else:
+                    psi_quant(1, int(tok[1]))
+            subtract(s)
+            exponent(s)
+            if s not in ON_VECTOR:
+                weigh(s)
+            for tok in steps.get(s, "").split():
+                u = int(tok[1:])
+                if tok[0] == "X":
+                    val_mx(u)
+                    val_mx(u + 1)
+                elif tok[0] == "R":
+                    sum_turn(u)
+                elif tok[0] == "N":
+                    empty_num(u)
+                else:
+                    empty(u, nc.scalar.copy)
+        weigh(14)
+        empty(4, nc.vector.tensor_copy)
+        weigh(15)
+        empty(5, nc.vector.tensor_copy)
+        for u in (12, 13, 14, 15):
+            sum_turn(u)
+        root(0, whole)
+        root(1, whole)
+        square(0, whole)
+        square(1, whole)
+        empty(6, nc.vector.tensor_copy)
+        normalise(0, whole)
+        root(2, whole)
+        normalise(1, whole)
+        empty(7, nc.vector.tensor_copy)
+        square(2, whole)
+        finish(0, whole)
+        root(3, whole)
+        finish(1, whole)
+        square(3, whole)
+        normalise(2, whole)
+        finish(2, whole)
+        normalise(3, whole)
+        finish(3, whole)

@@ -47,8 +47,8 @@ def tile_successor_feature_gpi_f1_kernel(
         x_t = [new("x_t%d" % i, [P, K], BF16) for i in range(4)]
         x_codes = new("x_codes", [P, 2, M], U32)
         x_plane = new("x_plane", [P, 2, M], U8)
-        w_perm = [new("w_perm%d" % i, [P, 2, 2 * W], U8) for i in range(3)]
-        plane_perm = [new("plane_perm%d" % i, [P, 2, W], U8) for i in range(3)]
+        w_perm = {i: new("w_perm%d" % i, [P, 2, 2 * W], U8) for i in (0, 1, 2, 5)}
+        plane_perm = {i: new("plane_perm%d" % i, [P, 2, W], U8) for i in (0, 1, 2, 5)}
         warm = new("warm", [P, W], BF16)
         phi_sb = [new("phi_sb%d" % g, [P, 4, W], BF16) for g in range(2)]
         phi_t = [new("phi_t%d" % g, [P, 4 * W], BF16) for g in range(2)]
@@ -58,13 +58,12 @@ def tile_successor_feature_gpi_f1_kernel(
         psi_plane = [new("psi_plane%d" % i, [P, 2, 2 * D], U8) for i in range(2)]
         pref_plane = new("pref_plane", [P, 2, T], U8)
         rows = new("rows", [P, 640], BF16)
-        rows_p = new("rows_p", [P, 640], BF16)
         consts = new("consts", [P, 5, 16], F32)
         dummy = new("dummy", [P, 8], F32)
         s_sb = [new("s_sb%d" % i, [P, 4 * W], F32) for i in range(4)]
         gate = [new("gate%d" % g, [P, 4 * W], F32) for g in range(2)]
         t1 = [new("t1_%d" % i, [P, 4 * W], F32) for i in range(2)]
-        psi_bf = [new("psi_bf%d" % i, [P, 4 * W], BF16) for i in range(4)]
+        psi_bf = new("psi_bf", [P, 4, 4 * W], BF16)
         psi_codes = [[new("psi_codes%d%d" % (g, i), [P, W], U32) for i in range(4)] for g in range(2)]
         psi_qplane = [[new("psi_qplane%d%d" % (g, i), [P, W], U8) for i in range(4)] for g in range(2)]
         best = [new("best%d" % i, [P, P], F32) for i in range(8)]
@@ -73,9 +72,8 @@ def tile_successor_feature_gpi_f1_kernel(
         wval = [s_sb[2 + i // 4][:, cols(i % 4, W)] for i in range(8)]
         num_sb = [gate[1][:, cols(i, W)] for i in range(2)]
         pair_sb = [new("pair_sb%d" % i, [P, 2, W], F32) for i in range(4)]
-        relu_sb = [new("relu_sb%d" % i, [P, W], F32) for i in range(3)]
-        rsq = [new("rsq%d" % i, [P, W], F32) for i in range(2)]
-        rec = [new("rec%d" % i, [P, W], F32) for i in range(2)]
+        relu_sb = [new("relu_sb%d" % i, [P, 2 * W], F32) for i in range(2)]
+        rec = [new("rec%d" % i, [P, W], F32) for i in range(4)]
         half = [new("half%d" % i, [P, W], F32) for i in range(2)]
         soft_out = [gate[0][:, cols(i, W)] for i in range(4)]
 
@@ -99,32 +97,32 @@ def tile_successor_feature_gpi_f1_kernel(
         def clear(eng, plane):
             eng.memset(plane[:].rearrange("p k n -> p (k n)").bitcast(U32), 0)
 
+        clear(nc.vector, gamma_plane)
         nc.vector.memset(rows[:], 0.0)
         nc.vector.memset(dummy[:], 0.0)
         nc.vector.memset(warm[:], 0.0)
-        clear(nc.vector, gamma_plane)
         clear(nc.vector, psi_plane[0])
         clear(nc.vector, psi_plane[1])
         clear(nc.vector, pref_plane)
+        nc.scalar.activation(out=dummy[:, 4:5], in_=dummy[:, 0:1], func=ACT.Sigmoid)
         make_identity(nc, ident[:])
+        nc.gpsimd.dma_start(out=rows[0:8, 0:W], in_=b_psi.rearrange("z (g c) -> (z g) c", g=2))
+        nc.gpsimd.dma_start(out=rows[8:10, 0:W], in_=b_gamma.rearrange("(g c) -> g c", g=2))
+        nc.gpsimd.dma_start(out=rows[0:4, W : W + P], in_=beta.rearrange("(a c) -> a c", a=4))
         make_identity(nc, ident_bf[:])
 
         nc.sync.dma_start(out=x_sb[0][:], in_=x[cols(0, P), :])
         nc.sync.dma_start(out=x_sb[1][:], in_=x[cols(1, P), :])
+        load_scales(gamma_plane, gamma_scales, 0, D)
         nc.sync.dma_start(out=x_sb[2][:], in_=x[cols(2, P), :])
         nc.sync.dma_start(out=x_sb[3][:], in_=x[cols(3, P), :])
-        nc.scalar.dma_start(out=rows[0:8, 0:W], in_=b_psi.rearrange("z (g c) -> (z g) c", g=2))
-        nc.scalar.dma_start(out=rows[8:10, 0:W], in_=b_gamma.rearrange("(g c) -> g c", g=2))
-        nc.scalar.dma_start(out=rows[0:4, W : W + P], in_=beta.rearrange("(a c) -> a c", a=4))
-        nc.scalar.activation(out=dummy[:, 4:5], in_=dummy[:, 0:1], func=ACT.Sigmoid)
         load_words(0)
-        load_scales(gamma_plane, gamma_scales, 0, D)
         load_scales(psi_plane[0], psi_scales, 0, 2 * D)
         load_words(1)
         load_words(2)
         load_phi(0)
         load_scales(psi_plane[1], psi_scales, 2 * D, Z * D)
-        for i in (3, 4, 5, 6):
+        for i in (3, 5, 4, 6):
             load_words(i)
         load_phi(1)
         for i in (7, 8, 9):
@@ -150,8 +148,9 @@ def tile_successor_feature_gpi_f1_kernel(
 
         def const_setup():
             view = bank[0][:].bitcast(BF16)
-            for j in range(5):
-                nc.tensor.transpose(view[:, cols(j, P)], rows_p[:, cols(j, P)], ident_bf[:])
+            for t in range(4):
+                nc.tensor.transpose(view[:, cols(t, P)], rows[:, t:W:4], ident_bf[:])
+            nc.tensor.transpose(view[:, cols(4, P)], rows[:, W : W + P], ident_bf[:])
             nc.scalar.copy(out=consts[:], in_=view[:, 0 : 5 * P].rearrange("p (j c) -> p j c", j=5)[:, :, 0:16])
 
         def w_plane(i):
@@ -174,9 +173,7 @@ def tile_successor_feature_gpi_f1_kernel(
 
         warm_up(4)
         x_transpose(0)
-        nc.vector.tensor_copy(out=rows_p[:, 0:W].rearrange("p (t c) -> p t c", t=4),
-                              in_=rows[:, 0:W].rearrange("p (c t) -> p t c", t=4))
-        nc.vector.tensor_copy(out=rows_p[:, W : W + P], in_=rows[:, W : W + P])
+        permute_scales(0)
         x_transpose(1)
         x_quant(0)
         x_transpose(2)
@@ -184,32 +181,34 @@ def tile_successor_feature_gpi_f1_kernel(
         permute_words(0, 0)
         x_transpose(3)
         const_setup()
-        warm_up(3)
-        x_quant(2)
+        warm_up(2)
         permute_words(0, 1)
+        x_quant(2)
         x_quant(3)
-        permute_scales(0)
         permute_scales(1)
         permute_words(1, 0)
         permute_words(1, 1)
 
-        count = {"mx": 1, "tr": 0, "relu": 0}
-        OFFLOAD = []
+        count = {"mx": 1, "tr": 0}
 
         def take(kind):
             b = bank[count[kind] % 4 + (0 if kind == "mx" else 4)]
             count[kind] += 1
             return b
 
-        def stage1_mx(i, h):
-            for a in (2 * h, 2 * h + 1):
-                acc = take("mx")
-                for k in range(2):
-                    nc.tensor.matmul_mx(
-                        out=acc[:], lhsT=x_codes[:, k, cols(a, P)].bitcast(FP8X4), lhsT_scale=x_plane[:, k, cols(a, P)],
-                        rhs=w_sb[i][:, k, :].bitcast(FP4X4), rhs_scale=w_plane(i)[:, k, :], start=(k == 0), stop=(k == 1))
-                nc.scalar.copy(out=s_sb[i % 4][:, cols(a, W)].rearrange("q (t p) -> q t p", t=4),
-                               in_=acc[:].rearrange("q (p t) -> q t p", t=4))
+        sums = {}
+
+        def stage1_mx(i, a):
+            acc = take("mx")
+            sums[(i, a)] = acc
+            for k in range(2):
+                nc.tensor.matmul_mx(
+                    out=acc[:], lhsT=x_codes[:, k, cols(a, P)].bitcast(FP8X4), lhsT_scale=x_plane[:, k, cols(a, P)],
+                    rhs=w_sb[i][:, k, :].bitcast(FP4X4), rhs_scale=w_plane(i)[:, k, :], start=(k == 0), stop=(k == 1))
+
+        def stage1_exit(i, a):
+            nc.scalar.copy(out=s_sb[i % 4][:, cols(a, W)].rearrange("q (t p) -> q t p", t=4),
+                           in_=sums[(i, a)][:].rearrange("q (p t) -> q t p", t=4))
 
         def phi_turn(g, eng_copy):
             for h in range(2):
@@ -220,84 +219,74 @@ def tile_successor_feature_gpi_f1_kernel(
                         nc.tensor.transpose(b[:, cols(2 * a + u, P)], words[:, u:256:2], ident[:])
                 word_copy(eng_copy, phi_t[g][:, cols(h, 2 * W)], b[:])
 
-        def psi_index(i):
-            z, g = groups[i]
-            return 4 * g + z
+        def gated(n, a0, a1):
+            return t1[n % 2][:].rearrange("p (t a m) -> p a m t", t=4, a=4)[:, a0:a1, :, :]
 
-        def finish_psi(n, a):
+        def finish_psi(n, a0, a1):
             g, z = divmod(n, 4)
-            if (n, a) in OFFLOAD:
-                r = relu_sb[count["relu"] % 3]
-                count["relu"] += 1
-                nc.scalar.activation(out=r[:].rearrange("p (m t) -> p m t", t=4),
-                                     in_=t1[n % 2][:].rearrange("p (t m) -> p m t", t=4)[:, cols(a, P), :], func=ACT.Relu)
-                nc.gpsimd.tensor_tensor(out=psi_bf[a][:, cols(z, W)], in0=r[:], in1=phi_t[g][:, cols(a, W)], op=ALU.add)
-                return
             nc.vector.scalar_tensor_tensor(
-                out=psi_bf[a][:, cols(z, W)].rearrange("p (m t) -> p m t", t=4),
-                in0=t1[n % 2][:].rearrange("p (t m) -> p m t", t=4)[:, cols(a, P), :],
-                scalar=0.0,
-                in1=phi_t[g][:, cols(a, W)].rearrange("p (m t) -> p m t", t=4),
-                op0=ALU.max, op1=ALU.add)
+                out=psi_bf[:, a0:a1, cols(z, W)].rearrange("p a (m t) -> p a m t", t=4), in0=gated(n, a0, a1), scalar=0.0,
+                in1=phi_t[g][:].rearrange("p (a m t) -> p a m t", a=4, t=4)[:, a0:a1, :, :], op0=ALU.max, op1=ALU.add)
+
+        def relu_aside(n):
+            nc.scalar.activation(out=relu_sb[n % 2][:].rearrange("p (a m t) -> p a m t", a=2, t=4), in_=gated(n, 0, 2), func=ACT.Relu)
+
+        def add_aside(n):
+            g, z = divmod(n, 4)
+            r = relu_sb[n % 2]
+            nc.gpsimd.tensor_tensor(out=psi_bf[:, 0:2, cols(z, W)], in0=r[:].rearrange("p (a c) -> p a c", a=2),
+                                    in1=phi_t[g][:, 0 : 2 * W].rearrange("p (a c) -> p a c", a=2), op=ALU.add)
 
         def psi_quant(g, a):
-            nc.vector.quantize_mx(out=psi_codes[g][a][:].bitcast(FP8X4), scales=psi_qplane[g][a][:], in_=psi_bf[a][:])
+            nc.vector.quantize_mx(out=psi_codes[g][a][:].bitcast(FP8X4), scales=psi_qplane[g][a][:], in_=psi_bf[:, a, :])
 
-        def consume(i, t, b):
+        held = {}
+
+        def consume(i, t):
             z, g = groups[i]
+            b = held[(i, t)]
             if z is None:
                 nc.scalar.activation(out=gate[g][:, cols(t, W)], in_=b[:], func=ACT.Sigmoid,
                                      bias=consts[:, t, 8 + g : 9 + g])
                 return
-            n = 4 * g + z
             nc.vector.scalar_tensor_tensor(
-                out=t1[n % 2][:, cols(t, W)], in0=b[:], scalar=consts[:, t, 2 * z + g : 2 * z + g + 1],
+                out=t1[(4 * g + z) % 2][:, cols(t, W)], in0=b[:], scalar=consts[:, t, 2 * z + g : 2 * z + g + 1],
                 in1=gate[g][:, cols(t, W)], op0=ALU.add, op1=ALU.mult)
-            if n == 4 and t > 0:
-                psi_quant(0, t - 1)
-            if n == 5 and t == 0:
-                psi_quant(0, 3)
-            if 1 < n < 7 or (n == 7 and t == 1):
-                finish_psi(n - 1, t if n < 7 else 0)
 
         def stage1_turn(i, h):
-            taken = []
             for t in (2 * h, 2 * h + 1):
                 b = take("tr")
-                taken.append((t, b))
+                held[(i, t)] = b
                 for a in range(4):
                     nc.tensor.transpose(b[:, cols(a, P)], s_sb[i % 4][:, cols(4 * a + t, P)], ident[:])
-            for t, b in taken:
-                consume(i, t, b)
 
         def stage1_direct(i, t):
-            b = take("mx" if i == 0 else "tr")
+            b = take("mx" if groups[i][0] is None else "tr")
+            held[(i, t)] = b
             for k in range(2):
                 nc.tensor.matmul_mx(
                     out=b[:], lhsT=w_perm[i][:, k, cols(t, 2 * P)].bitcast(FP4X4), lhsT_scale=plane_perm[i][:, k, cols(t, P)],
                     rhs=x_codes[:, k, :].bitcast(FP8X4), rhs_scale=x_plane[:, k, :], start=(k == 0), stop=(k == 1))
-            consume(i, t, b)
 
-        order = ("D00 D01 D10 S2 D02 D11 W20 D03 D12 W21 D13 P0 D20 F00 M3a D21 F01 M3b D22 F02 D23 F03 M4a "
-                 "T3a M4b T3b M5a M5b T4a M6a T5a T4b M6b T5b E "
-                 "T6a P1 M7a T6b M7b T7a M8a T7b M8b T8a M9a T8b M9b T9a T9b").split()
+        order = """
+            D00 C00 D01 C01 D10 C10 S2 D02 C02 D11 C11 W20 D03 C03 D12 C12 W21 D13 C13 S5 W50 W51 L0 P0 G0
+            D20 D21 M30 Z30 M31 Z31 D22 D23 M32 Z32 M33 Z33 C20 C21 C22 C23 M40 M41 T30 T31 L1 G1 Z40 Z41 F024
+            M42 M43 Z42 Z43 D50 D51 C30 C31 C32 C33 T40 T41 L2 G2 C50 C51 F124
+            M60 M61 Z60 Z61 M62 M63 Z62 Z63 D52 D53 C52 C53 C40 C41 C42 C43 M70 M71 T60 T61 L3 G3 Z70 Z71 F224
+            P1 M72 M73 Z72 Z73 C60 C61 C62 C63 T70 T71 Q00 Q01 L4 G4 F324
+            M80 M81 Z80 Z81 M82 M83 Z82 Z83 C70 C71 C72 C73 M90 M91 T80 T81 L5 G5 Z90 Z91 Q02 Q03 F424
+            M92 M93 Z92 Z93 C80 C81 C82 C83 T90 T91 L6 G6 F524
+            C90 C91 C92 C93 E F623
+        """.split()
         for tok in order:
+            n = [int(c) for c in tok[1:]]
             if tok == "E":
                 nc.scalar.activation(out=dummy[:, 5:6], in_=dummy[:, 0:1], func=ACT.Exp)
             elif tok[0] == "P":
-                phi_turn(int(tok[1]), nc.scalar.copy)
-            elif tok[0] == "S":
-                permute_scales(int(tok[1]))
-            elif tok[0] == "W":
-                permute_words(int(tok[1]), int(tok[2]))
-            elif tok[0] == "D":
-                stage1_direct(int(tok[1]), int(tok[2]))
-            elif tok[0] == "F":
-                finish_psi(int(tok[1]), int(tok[2]))
-            elif tok[0] == "M":
-                stage1_mx(int(tok[1]), "ab".index(tok[2]))
+                phi_turn(n[0], nc.scalar.copy)
             else:
-                stage1_turn(int(tok[1]), "ab".index(tok[2]))
+                {"S": permute_scales, "W": permute_words, "D": stage1_direct, "C": consume, "F": finish_psi,
+                 "L": relu_aside, "G": add_aside, "Q": psi_quant, "M": stage1_mx, "Z": stage1_exit, "T": stage1_turn}[tok[0]](*n)
 
         NUM = (4, 5)
         PAIR = (6, 7)
@@ -339,52 +328,51 @@ def tile_successor_feature_gpi_f1_kernel(
         def halves(ap, hs):
             return ap.rearrange("p (h c) -> p h c", h=2)[:, hs, :]
 
-        def empty(v, eng_copy):
+        def empty_best(v, eng_copy):
             a, h = divmod(v, 2)
-            eng_copy(out=pair_sb[a][:, h, :], in_=bank[PAIR[h]][:])
-            nc.sync.dma_start(out=out_0[cols(a, P), cols(h, 256)], in_=pair_sb[a][:, h, 0:256])
+            eng_copy(out=pair_sb[a][:, h, 0:256], in_=bank[PAIR[h]][:, 0:256])
+            if h == 1:
+                nc.sync.dma_start(out=halves(out_0[cols(a, P), :], slice(0, 2)), in_=pair_sb[a][:, :, 0:256])
+
+        def empty_den(v):
+            a, h = divmod(v, 2)
+            nc.scalar.activation(out=pair_sb[a][:, h, 256:W], in_=bank[PAIR[h]][:, 256:W], func=ACT.Square)
 
         def empty_num(a):
             nc.scalar.copy(out=num_sb[a], in_=bank[NUM[a]][:])
 
-        def root(a, hs):
-            nc.scalar.activation(out=halves(rsq[a % 2][:], hs), in_=pair_sb[a][:, hs, 256:W], func=ACT.Abs_reciprocal_sqrt)
-
-        def square(a, hs):
-            nc.scalar.activation(out=halves(rec[a % 2][:], hs), in_=halves(rsq[a % 2][:], hs), func=ACT.Square)
+        def invert(a, hs):
+            nc.scalar.activation(out=halves(rec[a][:], hs), in_=pair_sb[a][:, hs, 256:W], func=ACT.Abs_reciprocal_sqrt)
 
         def normalise(a, hs):
             num = num_sb[a] if a < 2 else bank[NUM[a % 2]][:]
-            nc.vector.tensor_tensor(out=halves(half[a % 2][:], hs), in0=halves(num, hs), in1=halves(rec[a % 2][:], hs), op=ALU.mult)
+            nc.vector.tensor_tensor(out=halves(half[a % 2][:], hs), in0=halves(num, hs), in1=halves(rec[a][:], hs), op=ALU.mult)
 
         def finish(a, hs):
             nc.vector.tensor_tensor(out=halves(soft_out[a], hs), in0=halves(half[a % 2][:], hs), in1=pair_sb[a][:, hs, 0:256], op=ALU.add)
             nc.sync.dma_start(out=halves(out_1[cols(a, P), :], hs), in_=halves(soft_out[a], hs))
 
-        ON_VECTOR = (14, 15)
-        whole = slice(0, 2)
+        ON_VECTOR = (15,)
+        whole, front, back = slice(0, 2), slice(0, 1), slice(1, 2)
         for u in range(4):
             val_mx(u, (0,))
-        finish_psi(6, 1)
-        finish_psi(7, 0)
-        finish_psi(7, 1)
+        finish_psi(7, 0, 1)
+        finish_psi(7, 1, 2)
         psi_quant(1, 0)
         for u in range(4):
             val_mx(u, (1,))
         psi_quant(1, 1)
-        finish_psi(6, 2)
+        finish_psi(6, 3, 4)
         max_all(0)
-        extra = {0: "F72", 1: "F63", 2: "Q2", 3: "F73", 5: "Q3"}
+        extra = {0: "F724", 2: "Q12", 4: "Q13"}
         steps = {1: "X4 R0", 3: "X6 R1 R2", 5: "E0 X8 R3 R4", 7: "E1 X10 R5", 8: "N0", 9: "E2 X12 R6 R7",
-                 11: "E3 X14 R8", 12: "N1 R9", 13: "R10", 14: "R11"}
+                 11: "E3 X14 R8", 12: "N1 R9", 13: "R10 E4", 14: "R11"}
         for s in range(16):
             if s + 1 < 16:
                 max_all(s + 1)
-            for tok in extra.get(s, "").split():
-                if tok[0] == "F":
-                    finish_psi(int(tok[1]), int(tok[2]))
-                else:
-                    psi_quant(1, int(tok[1]))
+            if s in extra:
+                n = [int(c) for c in extra[s][1:]]
+                {"F": finish_psi, "Q": psi_quant}[extra[s][0]](*n)
             subtract(s)
             exponent(s)
             if s not in ON_VECTOR:
@@ -399,28 +387,28 @@ def tile_successor_feature_gpi_f1_kernel(
                 elif tok[0] == "N":
                     empty_num(u)
                 else:
-                    empty(u, nc.scalar.copy)
-        weigh(14)
-        empty(4, nc.vector.tensor_copy)
+                    empty_den(u)
+                    empty_best(u, nc.scalar.copy)
+        sum_turn(12)
+        sum_turn(13)
+        empty_best(5, nc.vector.tensor_copy)
         weigh(15)
-        empty(5, nc.vector.tensor_copy)
-        for u in (12, 13, 14, 15):
-            sum_turn(u)
-        root(0, whole)
-        root(1, whole)
-        square(0, whole)
-        square(1, whole)
-        empty(6, nc.vector.tensor_copy)
+        invert(0, whole)
+        empty_den(5)
+        sum_turn(14)
+        sum_turn(15)
+        invert(1, whole)
         normalise(0, whole)
-        root(2, whole)
+        empty_den(6)
+        invert(2, whole)
         normalise(1, whole)
-        empty(7, nc.vector.tensor_copy)
-        square(2, whole)
         finish(0, whole)
-        root(3, whole)
+        empty_den(7)
+        invert(3, whole)
         finish(1, whole)
-        square(3, whole)
+        empty_best(6, nc.scalar.copy)
+        empty_best(7, nc.scalar.copy)
         normalise(2, whole)
-        finish(2, whole)
         normalise(3, whole)
+        finish(2, whole)
         finish(3, whole)

@@ -43,15 +43,16 @@ def tile_successor_feature_gpi_f1_kernel(
 
         ident = new("ident", [P, P], F32)
         ident_bf = new("ident_bf", [P, P], BF16)
-        x_sb = [new("x_sb%d" % i, [P, K], BF16) for i in range(4)]
-        x_t = [new("x_t%d" % i, [P, K], BF16) for i in range(4)]
+        x_all = new("x_all", [P, 8, K], BF16)
+        x_sb = [x_all[:, i, :] for i in range(4)]
+        x_t = [x_all[:, 4 + i, :] for i in range(4)]
         x_codes = new("x_codes", [P, 2, M], U32)
         x_plane = new("x_plane", [P, 2, M], U8)
-        w_perm = {i: new("w_perm%d" % i, [P, 2, 2 * W], U8) for i in (0, 1, 2, 5)}
-        plane_perm = {i: new("plane_perm%d" % i, [P, 2, W], U8) for i in (0, 1, 2, 5)}
+        w_perm = {i: new("w_perm%d" % i, [P, 2, 2 * W], U8) for i in (0, 1, 2, 3, 5)}
+        plane_perm = {i: new("plane_perm%d" % i, [P, 2, W], U8) for i in (0, 1, 2, 3, 5)}
         warm = new("warm", [P, W], BF16)
         phi_sb = [new("phi_sb%d" % g, [P, 4, W], BF16) for g in range(2)]
-        phi_t = [new("phi_t%d" % g, [P, 4 * W], BF16) for g in range(2)]
+        phi_t = [new("phi_t%d" % g, [P, 2 * W], BF16) for g in range(2)]
         w_sb = [new("w_sb%d" % i, [P, 2, 2 * W], U8) for i in range(10)]
         pref_sb = new("pref_sb", [P, 2, 2 * T], U8)
         gamma_plane = new("gamma_plane", [P, 2, D], U8)
@@ -67,7 +68,8 @@ def tile_successor_feature_gpi_f1_kernel(
         psi_codes = [[new("psi_codes%d%d" % (g, i), [P, W], U32) for i in range(4)] for g in range(2)]
         psi_qplane = [[new("psi_qplane%d%d" % (g, i), [P, W], U8) for i in range(4)] for g in range(2)]
         best = [new("best%d" % i, [P, P], F32) for i in range(8)]
-        diff = [tile[:].bitcast(F32) for tile in x_sb + x_t]
+        diff_all = x_all[:].rearrange("p a k -> p (a k)").bitcast(F32)
+        diff = [diff_all[:, cols(i, W)] for i in range(8)]
         expo = [s_sb[i // 4][:, cols(i % 4, W)] for i in range(8)]
         wval = [s_sb[2 + i // 4][:, cols(i % 4, W)] for i in range(8)]
         num_sb = [gate[1][:, cols(i, W)] for i in range(2)]
@@ -111,11 +113,11 @@ def tile_successor_feature_gpi_f1_kernel(
         nc.gpsimd.dma_start(out=rows[0:4, W : W + P], in_=beta.rearrange("(a c) -> a c", a=4))
         make_identity(nc, ident_bf[:])
 
-        nc.sync.dma_start(out=x_sb[0][:], in_=x[cols(0, P), :])
-        nc.sync.dma_start(out=x_sb[1][:], in_=x[cols(1, P), :])
+        nc.sync.dma_start(out=x_sb[0], in_=x[cols(0, P), :])
+        nc.sync.dma_start(out=x_sb[1], in_=x[cols(1, P), :])
         load_scales(gamma_plane, gamma_scales, 0, D)
-        nc.sync.dma_start(out=x_sb[2][:], in_=x[cols(2, P), :])
-        nc.sync.dma_start(out=x_sb[3][:], in_=x[cols(3, P), :])
+        nc.sync.dma_start(out=x_sb[2], in_=x[cols(2, P), :])
+        nc.sync.dma_start(out=x_sb[3], in_=x[cols(3, P), :])
         load_words(0)
         load_scales(psi_plane[0], psi_scales, 0, 2 * D)
         load_words(1)
@@ -135,11 +137,11 @@ def tile_successor_feature_gpi_f1_kernel(
                      in_=src.rearrange("p (a u m) -> p a m u", a=2, u=2))
 
         def x_transpose(a):
-            words = x_sb[a][:].bitcast(F32)
+            words = x_sb[a].bitcast(F32)
             for k in range(2):
                 for u in range(2):
                     nc.tensor.transpose(bank[4 + a][:, cols(2 * k + u, P)], words[:, 256 * k + u : 256 * (k + 1) : 2], ident[:])
-            word_copy(nc.scalar.copy, x_t[a][:], bank[4 + a][:])
+            word_copy(nc.scalar.copy, x_t[a], bank[4 + a][:])
 
         def x_quant(a):
             for k in range(2):
@@ -192,7 +194,7 @@ def tile_successor_feature_gpi_f1_kernel(
         count = {"mx": 1, "tr": 0}
 
         def take(kind):
-            b = bank[count[kind] % 4 + (0 if kind == "mx" else 4)]
+            b = bank[count[kind] % 3] if kind == "mx" else bank[4 + count[kind] % 4]
             count[kind] += 1
             return b
 
@@ -210,23 +212,33 @@ def tile_successor_feature_gpi_f1_kernel(
             nc.scalar.copy(out=s_sb[i % 4][:, cols(a, W)].rearrange("q (t p) -> q t p", t=4),
                            in_=sums[(i, a)][:].rearrange("q (p t) -> q t p", t=4))
 
-        def phi_turn(g, eng_copy):
-            for h in range(2):
-                b = take("mx")
+        phi_ps = bank[3][:].bitcast(BF16)
+
+        def phi_front(g):
+            b = take("mx")
+            for a in range(2):
+                words = phi_sb[g][:, a, :].bitcast(F32)
+                for u in range(2):
+                    nc.tensor.transpose(b[:, cols(2 * a + u, P)], words[:, u:256:2], ident[:])
+            word_copy(nc.scalar.copy, phi_t[g][:], b[:])
+
+        def phi_back(g):
+            for t in range(4):
                 for a in range(2):
-                    words = phi_sb[g][:, 2 * h + a, :].bitcast(F32)
-                    for u in range(2):
-                        nc.tensor.transpose(b[:, cols(2 * a + u, P)], words[:, u:256:2], ident[:])
-                word_copy(eng_copy, phi_t[g][:, cols(h, 2 * W)], b[:])
+                    nc.tensor.transpose(phi_ps[:, cols(2 * t + a, P)], phi_sb[g][:, 2 + a, t:W:4], ident_bf[:])
 
         def gated(n, a0, a1):
             return t1[n % 2][:].rearrange("p (t a m) -> p a m t", t=4, a=4)[:, a0:a1, :, :]
 
         def finish_psi(n, a0, a1):
             g, z = divmod(n, 4)
+            if a0 < 2:
+                now = phi_t[g][:].rearrange("p (a m t) -> p a m t", a=2, t=4)[:, a0:a1, :, :]
+            else:
+                now = phi_ps.rearrange("p (t a m) -> p a m t", t=4, a=2)[:, a0 - 2 : a1 - 2, :, :]
             nc.vector.scalar_tensor_tensor(
                 out=psi_bf[:, a0:a1, cols(z, W)].rearrange("p a (m t) -> p a m t", t=4), in0=gated(n, a0, a1), scalar=0.0,
-                in1=phi_t[g][:].rearrange("p (a m t) -> p a m t", a=4, t=4)[:, a0:a1, :, :], op0=ALU.max, op1=ALU.add)
+                in1=now, op0=ALU.max, op1=ALU.add)
 
         def relu_aside(n):
             nc.scalar.activation(out=relu_sb[n % 2][:].rearrange("p (a m t) -> p a m t", a=2, t=4), in_=gated(n, 0, 2), func=ACT.Relu)
@@ -235,7 +247,7 @@ def tile_successor_feature_gpi_f1_kernel(
             g, z = divmod(n, 4)
             r = relu_sb[n % 2]
             nc.gpsimd.tensor_tensor(out=psi_bf[:, 0:2, cols(z, W)], in0=r[:].rearrange("p (a c) -> p a c", a=2),
-                                    in1=phi_t[g][:, 0 : 2 * W].rearrange("p (a c) -> p a c", a=2), op=ALU.add)
+                                    in1=phi_t[g][:].rearrange("p (a c) -> p a c", a=2), op=ALU.add)
 
         def psi_quant(g, a):
             nc.vector.quantize_mx(out=psi_codes[g][a][:].bitcast(FP8X4), scales=psi_qplane[g][a][:], in_=psi_bf[:, a, :])
@@ -269,24 +281,22 @@ def tile_successor_feature_gpi_f1_kernel(
                     rhs=x_codes[:, k, :].bitcast(FP8X4), rhs_scale=x_plane[:, k, :], start=(k == 0), stop=(k == 1))
 
         order = """
-            D00 C00 D01 C01 D10 C10 S2 D02 C02 D11 C11 W20 D03 C03 D12 C12 W21 D13 C13 S5 W50 W51 L0 P0 G0
-            D20 D21 M30 Z30 M31 Z31 D22 D23 M32 Z32 M33 Z33 C20 C21 C22 C23 M40 M41 T30 T31 L1 G1 Z40 Z41 F024
-            M42 M43 Z42 Z43 D50 D51 C30 C31 C32 C33 T40 T41 L2 G2 C50 C51 F124
-            M60 M61 Z60 Z61 M62 M63 Z62 Z63 D52 D53 C52 C53 C40 C41 C42 C43 M70 M71 T60 T61 L3 G3 Z70 Z71 F224
-            P1 M72 M73 Z72 Z73 C60 C61 C62 C63 T70 T71 Q00 Q01 L4 G4 F324
-            M80 M81 Z80 Z81 M82 M83 Z82 Z83 C70 C71 C72 C73 M90 M91 T80 T81 L5 G5 Z90 Z91 Q02 Q03 F424
-            M92 M93 Z92 Z93 C80 C81 C82 C83 T90 T91 L6 G6 F524
-            C90 C91 C92 C93 E F623
+            D00 C00 D01 C01 D10 C10 S2 D02 C02 D11 C11 W20 D03 C03 D12 C12 W21 D13 C13 S3 W30 W31 L0 P0 G0
+            D20 D21 D22 D23 B0 M40 Z40 M41 Z41 C20 C21 C22 C23 D30 D31 D32 D33 L1 G1 F024 S5 W50
+            M42 M43 Z42 Z43 M60 Z60 C30 C31 C32 C33 T40 T41 L2 G2 F124 W51
+            M61 Z61 M62 M63 Z62 Z63 D50 D51 C50 C51 C40 C41 D52 D53 C52 C53 C42 C43 T60 T61 L3 G3 F224
+            P1 M70 Z70 M71 Z71 M72 M73 Z72 Z73 C60 C61 C62 C63 M80 T70 T71 L4 Z80 F324 Q00 Q01 G4 Q02 Q03
+            M81 Z81 M82 M83 Z82 Z83 B1 C70 C71 C72 C73 M90 T80 T81 L5 G5 Z90 F424
+            M91 Z91 M92 M93 Z92 Z93 C80 C81 C82 C83 T90 T91 L6 G6 F524
+            C90 C91 C92 C93 E F624
         """.split()
         for tok in order:
             n = [int(c) for c in tok[1:]]
             if tok == "E":
                 nc.scalar.activation(out=dummy[:, 5:6], in_=dummy[:, 0:1], func=ACT.Exp)
-            elif tok[0] == "P":
-                phi_turn(n[0], nc.scalar.copy)
             else:
                 {"S": permute_scales, "W": permute_words, "D": stage1_direct, "C": consume, "F": finish_psi,
-                 "L": relu_aside, "G": add_aside, "Q": psi_quant, "M": stage1_mx, "Z": stage1_exit, "T": stage1_turn}[tok[0]](*n)
+                 "P": phi_front, "B": phi_back, "L": relu_aside, "G": add_aside, "Q": psi_quant, "M": stage1_mx, "Z": stage1_exit, "T": stage1_turn}[tok[0]](*n)
 
         NUM = (4, 5)
         PAIR = (6, 7)
@@ -312,9 +322,9 @@ def tile_successor_feature_gpi_f1_kernel(
             j = u % 4
             nc.scalar.activation(out=expo[u % 8], in_=diff[u % 8], func=ACT.Exp, scale=consts[:, 4, j : j + 1])
 
-        def weigh(u):
-            eng = nc.vector if u in ON_VECTOR else nc.gpsimd
-            eng.tensor_tensor(out=wval[u % 8], in0=diff[u % 8], in1=expo[u % 8], op=ALU.mult)
+        def weigh(eng, u0, u1):
+            q, c = u0 % 8 // 4, slice(u0 % 4 * W, (u0 % 4 + u1 - u0) * W)
+            eng.tensor_tensor(out=s_sb[2 + q][:, c], in0=diff_all[:, u0 % 8 * W : (u0 % 8 + u1 - u0) * W], in1=s_sb[q][:, c], op=ALU.mult)
 
         def sum_turn(u):
             a, j = divmod(u, 4)
@@ -352,21 +362,22 @@ def tile_successor_feature_gpi_f1_kernel(
             nc.vector.tensor_tensor(out=halves(soft_out[a], hs), in0=halves(half[a % 2][:], hs), in1=pair_sb[a][:, hs, 0:256], op=ALU.add)
             nc.sync.dma_start(out=halves(out_1[cols(a, P), :], hs), in_=halves(soft_out[a], hs))
 
-        ON_VECTOR = (15,)
+        spans = {0: 0, 1: 1, 3: 2, 5: 4, 7: 6, 9: 8, 11: 10, 13: 12}
         whole, front, back = slice(0, 2), slice(0, 1), slice(1, 2)
-        for u in range(4):
+        for u in range(3):
             val_mx(u, (0,))
         finish_psi(7, 0, 1)
         finish_psi(7, 1, 2)
         psi_quant(1, 0)
-        for u in range(4):
+        for u in range(3):
             val_mx(u, (1,))
+        finish_psi(7, 2, 4)
+        val_mx(3)
         psi_quant(1, 1)
-        finish_psi(6, 3, 4)
         max_all(0)
-        extra = {0: "F724", 2: "Q12", 4: "Q13"}
-        steps = {1: "X4 R0", 3: "X6 R1 R2", 5: "E0 X8 R3 R4", 7: "E1 X10 R5", 8: "N0", 9: "E2 X12 R6 R7",
-                 11: "E3 X14 R8", 12: "N1 R9", 13: "R10 E4", 14: "R11"}
+        extra = {0: "Q12", 1: "Q13"}
+        steps = {1: "X4 R0", 3: "X6 R1", 5: "X8 R2 E0 R3", 7: "X10 R4 E1 R5", 8: "N0", 9: "X12 R6 E2 R7",
+                 11: "X14 R8 E3 R9", 12: "N1", 13: "R10 E4 R11"}
         for s in range(16):
             if s + 1 < 16:
                 max_all(s + 1)
@@ -375,8 +386,8 @@ def tile_successor_feature_gpi_f1_kernel(
                 {"F": finish_psi, "Q": psi_quant}[extra[s][0]](*n)
             subtract(s)
             exponent(s)
-            if s not in ON_VECTOR:
-                weigh(s)
+            if s in spans:
+                weigh(nc.gpsimd, spans[s], s + 1)
             for tok in steps.get(s, "").split():
                 u = int(tok[1:])
                 if tok[0] == "X":
@@ -391,8 +402,9 @@ def tile_successor_feature_gpi_f1_kernel(
                     empty_best(u, nc.scalar.copy)
         sum_turn(12)
         sum_turn(13)
+        weigh(nc.vector, 14, 15)
         empty_best(5, nc.vector.tensor_copy)
-        weigh(15)
+        weigh(nc.vector, 15, 16)
         invert(0, whole)
         empty_den(5)
         sum_turn(14)

from contextlib import ExitStack

import concourse.mybir as mybir
from concourse.masks import make_identity

M, K, Z, D, T = 512, 1024, 4, 1024, 512
FLOPS = 2 * M * K * (Z * D + D) + 2 * M * Z * D * T

F32 = mybir.dt.float32
BF16 = mybir.dt.bfloat16
I32 = mybir.dt.int32
U32 = mybir.dt.uint32
U8 = mybir.dt.uint8
FP8X4 = mybir.dt.float8_e4m3fn_x4
FP4X4 = mybir.dt.float4_e2m1fn_x4
ALU = mybir.AluOpType
ACT = mybir.ActivationFunctionType

P = 128
W = 512


def cols(i, n):
    return slice(i * n, (i + 1) * n)


def tile_successor_feature_gpi_f1_kernel(
    tc, x, phi, psi_words, psi_scales, b_psi, gamma_words, gamma_scales, b_gamma,
    pref_words, pref_scales, beta, out_0, out_1,
):
    nc = tc.nc
    with ExitStack() as ctx:
        sb = ctx.enter_context(tc.tile_pool(name="sb", bufs=1))
        ps = ctx.enter_context(tc.psum_pool(name="ps", bufs=1))
        ctx.enter_context(tc.manual_schedule())

        def new(name, shape, dtype):
            return sb.tile(shape, dtype, name=name, align_bytes=64)

        bank = [ps.tile([P, W], F32, name="bank%d" % i) for i in range(8)]

        groups = [(None, 0), (0, 0), (1, 0), (2, 0), (3, 0), (None, 1), (0, 1), (1, 1), (2, 1), (3, 1)]

        ident = new("ident", [P, P], F32)
        ident_bf = new("ident_bf", [P, P], BF16)
        x_all = new("x_all", [P, 8, K], BF16)
        x_sb = [x_all[:, i, :] for i in range(4)]
        x_t = [x_all[:, 4 + i, :] for i in range(4)]
        x_codes = new("x_codes", [P, 2, M], U32)
        x_plane = new("x_plane", [P, 2, M], U8)
        w_perm = {i: new("w_perm%d" % i, [P, 2, 2 * W], U8) for i in (0, 1, 2, 3, 5)}
        plane_perm = {i: new("plane_perm%d" % i, [P, 2, W], U8) for i in (0, 1, 2, 3, 5)}
        warm = new("warm", [P, W], BF16)
        phi_sb = [new("phi_sb%d" % g, [P, 4, W], BF16) for g in range(2)]
        phi_t = [new("phi_t%d" % g, [P, 2 * W], BF16) for g in range(2)]
        w_sb = [new("w_sb%d" % i, [P, 2, 2 * W], U8) for i in range(10)]
        pref_sb = new("pref_sb", [P, 2, 2 * T], U8)
        gamma_plane = new("gamma_plane", [P, 2, D], U8)
        psi_plane = [new("psi_plane%d" % i, [P, 2, 2 * D], U8) for i in range(2)]
        pref_plane = new("pref_plane", [P, 2, T], U8)
        rows = new("rows", [P, 640], BF16)
        consts = new("consts", [P, 5, 16], F32)
        dummy = new("dummy", [P, 8], F32)
        s_sb = [new("s_sb%d" % i, [P, 4 * W], F32) for i in range(4)]
        gate = [new("gate%d" % g, [P, 4 * W], F32) for g in range(2)]
        t1 = [new("t1_%d" % i, [P, 4 * W], F32) for i in range(2)]
        psi_bf = new("psi_bf", [P, 4, 4 * W], BF16)
        psi_codes = [[new("psi_codes%d%d" % (g, i), [P, W], U32) for i in range(4)] for g in range(2)]
        psi_qplane = [[new("psi_qplane%d%d" % (g, i), [P, W], U8) for i in range(4)] for g in range(2)]
        best = [new("best%d" % i, [P, P], F32) for i in range(8)]
        diff_all = x_all[:].rearrange("p a k -> p (a k)").bitcast(F32)
        diff = [diff_all[:, cols(i, W)] for i in range(8)]
        expo = [s_sb[i // 4][:, cols(i % 4, W)] for i in range(8)]
        wval = [s_sb[2 + i // 4][:, cols(i % 4, W)] for i in range(8)]
        num_sb = [gate[1][:, cols(i, W)] for i in range(2)]
        pair_sb = [new("pair_sb%d" % i, [P, 2, W], F32) for i in range(4)]
        relu_sb = [new("relu_sb%d" % i, [P, 2 * W], F32) for i in range(2)]
        rec = [new("rec%d" % i, [P, W], F32) for i in range(4)]
        half = [new("half%d" % i, [P, W], F32) for i in range(2)]
        soft_out = [gate[0][:, cols(i, W)] for i in range(4)]

        def load_scales(plane, src, c0, c1):
            view = src.bitcast(I32).rearrange("k (q r) n -> r q k n", r=4)
            for r in range(4):
                nc.sync.dma_start(out=plane[r:P:32, :, :].bitcast(I32), in_=view[r][:, :, c0 // 4 : c1 // 4])

        def load_words(i):
            z, g = groups[i]
            if z is None:
                src, c0 = gamma_words, g * W
            else:
                src, c0 = psi_words, z * D + g * W
            view = src.bitcast(I32).rearrange("k p n -> p k n")
            nc.sync.dma_start(out=w_sb[i][:].bitcast(I32), in_=view[:, :, c0 // 2 : (c0 + W) // 2])

        def load_phi(g):
            nc.sync.dma_start(out=phi_sb[g][:], in_=phi[:, cols(g, W)].rearrange("(a p) c -> p a c", p=P))

        def clear(eng, plane):
            eng.memset(plane[:].rearrange("p k n -> p (k n)").bitcast(U32), 0)

        clear(nc.vector, gamma_plane)
        nc.vector.memset(rows[:], 0.0)
        nc.vector.memset(dummy[:], 0.0)
        nc.vector.memset(warm[:], 0.0)
        clear(nc.vector, psi_plane[0])
        clear(nc.vector, psi_plane[1])
        clear(nc.vector, pref_plane)
        nc.scalar.activation(out=dummy[:, 4:5], in_=dummy[:, 0:1], func=ACT.Sigmoid)
        make_identity(nc, ident[:])
        nc.gpsimd.dma_start(out=rows[0:8, 0:W], in_=b_psi.rearrange("z (g c) -> (z g) c", g=2))
        nc.gpsimd.dma_start(out=rows[8:10, 0:W], in_=b_gamma.rearrange("(g c) -> g c", g=2))
        nc.gpsimd.dma_start(out=rows[0:4, W : W + P], in_=beta.rearrange("(a c) -> a c", a=4))
        make_identity(nc, ident_bf[:])

        nc.sync.dma_start(out=x_sb[0], in_=x[cols(0, P), :])
        nc.sync.dma_start(out=x_sb[1], in_=x[cols(1, P), :])
        load_scales(gamma_plane, gamma_scales, 0, D)
        nc.sync.dma_start(out=x_sb[2], in_=x[cols(2, P), :])
        nc.sync.dma_start(out=x_sb[3], in_=x[cols(3, P), :])
        load_words(0)
        load_scales(psi_plane[0], psi_scales, 0, 2 * D)
        load_words(1)
        load_words(2)
        load_phi(0)
        load_scales(psi_plane[1], psi_scales, 2 * D, Z * D)
        for i in (3, 5, 4, 6):
            load_words(i)
        load_phi(1)
        for i in (7, 8, 9):
            load_words(i)
        load_scales(pref_plane, pref_scales, 0, T)
        nc.sync.dma_start(out=pref_sb[:].bitcast(I32), in_=pref_words.bitcast(I32).rearrange("k p n -> p k n"))

        def word_copy(eng_copy, dst, src):
            eng_copy(out=dst.bitcast(F32).rearrange("p (a m u) -> p a m u", a=2, u=2),
                     in_=src.rearrange("p (a u m) -> p a m u", a=2, u=2))

        def x_transpose(a):
            words = x_sb[a].bitcast(F32)
            for k in range(2):
                for u in range(2):
                    nc.tensor.transpose(bank[4 + a][:, cols(2 * k + u, P)], words[:, 256 * k + u : 256 * (k + 1) : 2], ident[:])
            word_copy(nc.scalar.copy, x_t[a], bank[4 + a][:])

        def x_quant(a):
            for k in range(2):
                nc.vector.quantize_mx(out=x_codes[:, k, cols(a, P)].bitcast(FP8X4), scales=x_plane[:, k, cols(a, P)],
                                      in_=x_t[a][:, cols(k, W)])

        def const_setup():
            view = bank[0][:].bitcast(BF16)
            for t in range(4):
                nc.tensor.transpose(view[:, cols(t, P)], rows[:, t:W:4], ident_bf[:])
            nc.tensor.transpose(view[:, cols(4, P)], rows[:, W : W + P], ident_bf[:])
            nc.scalar.copy(out=consts[:], in_=view[:, 0 : 5 * P].rearrange("p (j c) -> p j c", j=5)[:, :, 0:16])

        def w_plane(i):
            z, g = groups[i]
            if z is None:
                return gamma_plane[:, :, cols(g, W)]
            return psi_plane[z // 2][:, :, cols(2 * (z % 2) + g, W)]

        def permute_words(i, k):
            nc.vector.tensor_copy(out=w_perm[i][:, k, :].rearrange("p (t c b) -> p t c b", t=4, b=2),
                                  in_=w_sb[i][:, k, :].rearrange("p (c t b) -> p t c b", t=4, b=2))

        def permute_scales(i):
            nc.vector.tensor_copy(out=plane_perm[i][:].rearrange("p k (t c) -> p k t c", t=4),
                                  in_=w_plane(i).rearrange("p k (c t) -> p k t c", t=4))

        def warm_up(n):
            for j in range(n):
                nc.tensor.matmul(out=bank[1][:], lhsT=warm[:, 0:P], rhs=warm[:], start=True, stop=True)

        warm_up(4)
        x_transpose(0)
        permute_scales(0)
        x_transpose(1)
        x_quant(0)
        x_transpose(2)
        x_quant(1)
        permute_words(0, 0)
        x_transpose(3)
        const_setup()
        warm_up(2)
        permute_words(0, 1)
        x_quant(2)
        x_quant(3)
        permute_scales(1)
        permute_words(1, 0)
        permute_words(1, 1)

        count = {"mx": 1, "tr": 0}

        def take(kind):
            b = bank[count[kind] % 3] if kind == "mx" else bank[4 + count[kind] % 4]
            count[kind] += 1
            return b

        sums = {}

        def stage1_mx(i, a):
            acc = take("mx")
            sums[(i, a)] = acc
            for k in range(2):
                nc.tensor.matmul_mx(
                    out=acc[:], lhsT=x_codes[:, k, cols(a, P)].bitcast(FP8X4), lhsT_scale=x_plane[:, k, cols(a, P)],
                    rhs=w_sb[i][:, k, :].bitcast(FP4X4), rhs_scale=w_plane(i)[:, k, :], start=(k == 0), stop=(k == 1))

        def stage1_exit(i, a):
            nc.scalar.copy(out=s_sb[i % 4][:, cols(a, W)].rearrange("q (t p) -> q t p", t=4),
                           in_=sums[(i, a)][:].rearrange("q (p t) -> q t p", t=4))

        phi_ps = bank[3][:].bitcast(BF16)

        def phi_front(g):
            b = take("mx")
            for a in range(2):
                words = phi_sb[g][:, a, :].bitcast(F32)
                for u in range(2):
                    nc.tensor.transpose(b[:, cols(2 * a + u, P)], words[:, u:256:2], ident[:])
            word_copy(nc.scalar.copy, phi_t[g][:], b[:])

        def phi_back(g):
            for t in range(4):
                for a in range(2):
                    nc.tensor.transpose(phi_ps[:, cols(2 * t + a, P)], phi_sb[g][:, 2 + a, t:W:4], ident_bf[:])

        def gated(n, a0, a1):
            return t1[n % 2][:].rearrange("p (t a m) -> p a m t", t=4, a=4)[:, a0:a1, :, :]

        def finish_psi(n, a0, a1):
            g, z = divmod(n, 4)
            if a0 < 2:
                now = phi_t[g][:].rearrange("p (a m t) -> p a m t", a=2, t=4)[:, a0:a1, :, :]
            else:
                now = phi_ps.rearrange("p (t a m) -> p a m t", t=4, a=2)[:, a0 - 2 : a1 - 2, :, :]
            nc.vector.scalar_tensor_tensor(
                out=psi_bf[:, a0:a1, cols(z, W)].rearrange("p a (m t) -> p a m t", t=4), in0=gated(n, a0, a1), scalar=0.0,
                in1=now, op0=ALU.max, op1=ALU.add)

        def relu_aside(n):
            nc.scalar.activation(out=relu_sb[n % 2][:].rearrange("p (a m t) -> p a m t", a=2, t=4), in_=gated(n, 0, 2), func=ACT.Relu)

        def add_aside(n):
            g, z = divmod(n, 4)
            r = relu_sb[n % 2]
            nc.gpsimd.tensor_tensor(out=psi_bf[:, 0:2, cols(z, W)], in0=r[:].rearrange("p (a c) -> p a c", a=2),
                                    in1=phi_t[g][:].rearrange("p (a c) -> p a c", a=2), op=ALU.add)

        def psi_quant(g, a):
            nc.vector.quantize_mx(out=psi_codes[g][a][:].bitcast(FP8X4), scales=psi_qplane[g][a][:], in_=psi_bf[:, a, :])

        held = {}

        def consume(i, t):
            z, g = groups[i]
            b = held[(i, t)]
            if z is None:
                nc.scalar.activation(out=gate[g][:, cols(t, W)], in_=b[:], func=ACT.Sigmoid,
                                     bias=consts[:, t, 8 + g : 9 + g])
                return
            nc.vector.scalar_tensor_tensor(
                out=t1[(4 * g + z) % 2][:, cols(t, W)], in0=b[:], scalar=consts[:, t, 2 * z + g : 2 * z + g + 1],
                in1=gate[g][:, cols(t, W)], op0=ALU.add, op1=ALU.mult)

        def stage1_turn(i, h):
            for t in (2 * h, 2 * h + 1):
                b = take("tr")
                held[(i, t)] = b
                for a in range(4):
                    nc.tensor.transpose(b[:, cols(a, P)], s_sb[i % 4][:, cols(4 * a + t, P)], ident[:])

        def stage1_direct(i, t):
            b = take("mx" if groups[i][0] is None else "tr")
            held[(i, t)] = b
            for k in range(2):
                nc.tensor.matmul_mx(
                    out=b[:], lhsT=w_perm[i][:, k, cols(t, 2 * P)].bitcast(FP4X4), lhsT_scale=plane_perm[i][:, k, cols(t, P)],
                    rhs=x_codes[:, k, :].bitcast(FP8X4), rhs_scale=x_plane[:, k, :], start=(k == 0), stop=(k == 1))

        order = """
            D00 C00 D01 C01 D10 C10 S2 D02 C02 D11 C11 W20 D03 C03 D12 C12 W21 D13 C13 S3 W30 W31 L0 P0 G0
            D20 D21 D22 D23 B0 M40 Z40 M41 Z41 C20 C21 C22 C23 D30 D31 D32 D33 L1 G1 F024 S5 W50
            M42 M43 Z42 Z43 M60 Z60 C30 C31 C32 C33 T40 T41 L2 G2 F124 W51
            M61 Z61 M62 M63 Z62 Z63 D50 D51 C50 C51 C40 C41 D52 D53 C52 C53 C42 C43 T60 T61 L3 G3 F224
            P1 M70 Z70 M71 Z71 M72 M73 Z72 Z73 C60 C61 C62 C63 M80 T70 T71 L4 Z80 F324 Q00 Q01 G4 Q02 Q03
            M81 Z81 M82 M83 Z82 Z83 B1 C70 C71 C72 C73 M90 T80 T81 L5 G5 Z90 F424
            M91 Z91 M92 M93 Z92 Z93 C80 C81 C82 C83 T90 T91 L6 G6 F524
            C90 C91 C92 C93 E F624
        """.split()
        for tok in order:
            n = [int(c) for c in tok[1:]]
            if tok == "E":
                nc.scalar.activation(out=dummy[:, 5:6], in_=dummy[:, 0:1], func=ACT.Exp)
            else:
                {"S": permute_scales, "W": permute_words, "D": stage1_direct, "C": consume, "F": finish_psi,
                 "P": phi_front, "B": phi_back, "L": relu_aside, "G": add_aside, "Q": psi_quant, "M": stage1_mx, "Z": stage1_exit, "T": stage1_turn}[tok[0]](*n)

        NUM = (4, 5)
        PAIR = (6, 7)

        def val_mx(u, halves=(0, 1)):
            a, j = divmod(u, 4)
            for g in halves:
                nc.tensor.matmul_mx(
                    out=bank[u % 4][:], lhsT=pref_sb[:, g, cols(j, 2 * P)].bitcast(FP4X4), lhsT_scale=pref_plane[:, g, cols(j, P)],
                    rhs=psi_codes[g][a][:].bitcast(FP8X4), rhs_scale=psi_qplane[g][a][:], start=(g == 0), stop=(g == 1))

        def max_all(u):
            nc.vector.tensor_reduce(out=best[u % 8][:], in_=bank[u % 4][:].rearrange("p (z m) -> p m z", z=4),
                                    axis=mybir.AxisListType.X, op=ALU.max)

        def subtract(u):
            nc.vector.tensor_tensor(
                out=diff[u % 8].rearrange("p (z m) -> p z m", z=4),
                in0=bank[u % 4][:].rearrange("p (z m) -> p z m", z=4),
                in1=best[u % 8][:].unsqueeze(1).to_broadcast([P, 4, P]), op=ALU.subtract)

        def exponent(u):
            j = u % 4
            nc.scalar.activation(out=expo[u % 8], in_=diff[u % 8], func=ACT.Exp, scale=consts[:, 4, j : j + 1])

        def weigh(eng, u0, u1):
            q, c = u0 % 8 // 4, slice(u0 % 4 * W, (u0 % 4 + u1 - u0) * W)
            eng.tensor_tensor(out=s_sb[2 + q][:, c], in0=diff_all[:, u0 % 8 * W : (u0 % 8 + u1 - u0) * W], in1=s_sb[q][:, c], op=ALU.mult)

        def sum_turn(u):
            a, j = divmod(u, 4)
            pair = bank[PAIR[j // 2]]
            nc.tensor.transpose(pair[:, cols(j % 2, P)], best[u % 8][:], ident[:])
            for dst, src in ((pair[:, cols(2 + j % 2, P)], expo[u % 8]), (bank[NUM[a % 2]][:, cols(j, P)], wval[u % 8])):
                for z in range(4):
                    nc.tensor.matmul(out=dst, lhsT=src[:, cols(z, P)], rhs=ident[:],
                                     start=(z == 0), stop=(z == 3), is_transpose=True)

        def halves(ap, hs):
            return ap.rearrange("p (h c) -> p h c", h=2)[:, hs, :]

        def empty_best(v, eng_copy):
            a, h = divmod(v, 2)
            eng_copy(out=pair_sb[a][:, h, 0:256], in_=bank[PAIR[h]][:, 0:256])
            if h == 1:
                nc.sync.dma_start(out=halves(out_0[cols(a, P), :], slice(0, 2)), in_=pair_sb[a][:, :, 0:256])

        def empty_den(v):
            a, h = divmod(v, 2)
            nc.scalar.activation(out=pair_sb[a][:, h, 256:W], in_=bank[PAIR[h]][:, 256:W], func=ACT.Square)

        def empty_num(a):
            nc.scalar.copy(out=num_sb[a], in_=bank[NUM[a]][:])

        def invert(a, hs):
            nc.scalar.activation(out=halves(rec[a][:], hs), in_=pair_sb[a][:, hs, 256:W], func=ACT.Abs_reciprocal_sqrt)

        def normalise(a, hs):
            num = num_sb[a] if a < 2 else bank[NUM[a % 2]][:]
            nc.vector.tensor_tensor(out=halves(half[a % 2][:], hs), in0=halves(num, hs), in1=halves(rec[a][:], hs), op=ALU.mult)

        def finish(a, hs):
            nc.vector.tensor_tensor(out=halves(soft_out[a], hs), in0=halves(half[a % 2][:], hs), in1=pair_sb[a][:, hs, 0:256], op=ALU.add)
            nc.sync.dma_start(out=halves(out_1[cols(a, P), :], hs), in_=halves(soft_out[a], hs))

        spans = {0: 0, 1: 1, 3: 2, 5: 4, 7: 6, 9: 8, 11: 10, 13: 12}
        whole, front, back = slice(0, 2), slice(0, 1), slice(1, 2)
        for u in range(3):
            val_mx(u, (0,))
        finish_psi(7, 0, 1)
        finish_psi(7, 1, 2)
        psi_quant(1, 0)
        for u in range(3):
            val_mx(u, (1,))
        finish_psi(7, 2, 4)
        val_mx(3)
        psi_quant(1, 1)
        max_all(0)
        extra = {0: "Q12", 1: "Q13"}
        steps = {1: "X4 R0", 3: "X6 R1", 5: "X8 R2 E0 R3", 7: "X10 R4 E1 R5", 8: "N0", 9: "X12 R6 E2 R7",
                 11: "X14 R8 E3 R9", 12: "N1", 13: "R10 E4 R11"}
        for s in range(16):
            if s + 1 < 16:
                max_all(s + 1)
            if s in extra:
                n = [int(c) for c in extra[s][1:]]
                {"F": finish_psi, "Q": psi_quant}[extra[s][0]](*n)
            subtract(s)
            exponent(s)
            if s in spans:
                weigh(nc.gpsimd, spans[s], s + 1)
            for tok in steps.get(s, "").split():
                u = int(tok[1:])
                if tok[0] == "X":
                    val_mx(u)
                    val_mx(u + 1)
                elif tok[0] == "R":
                    sum_turn(u)
                elif tok[0] == "N":
                    empty_num(u)
                else:
                    empty_den(u)
                    empty_best(u, nc.scalar.copy)
        sum_turn(12)
        sum_turn(13)
        weigh(nc.vector, 14, 15)
        empty_best(5, nc.vector.tensor_copy)
        weigh(nc.vector, 15, 16)
        invert(0, whole)
        empty_den(5)
        sum_turn(14)
        sum_turn(15)
        invert(1, whole)
        normalise(0, whole)
        empty_den(6)
        invert(2, whole)
        normalise(1, whole)
        finish(0, whole)
        empty_den(7)
        invert(3, whole)
        finish(1, whole)
        empty_best(6, nc.scalar.copy)
        empty_best(7, nc.scalar.copy)
        normalise(2, whole)
        normalise(3, whole)
        finish(2, whole)
        finish(3, whole)
